import numpy as np
import ml_dtypes


def mxq(x, axis, fmt="e4m3"):
    dtype, down = {"e4m3": (ml_dtypes.float8_e4m3fn, 7), "e5m2": (ml_dtypes.float8_e5m2, 14)}[fmt]
    v = np.moveaxis(np.asarray(x, np.float32).astype(ml_dtypes.bfloat16).astype(np.float64), axis, -1)
    blocks = v.reshape(v.shape[:-1] + (-1, 32))
    amax = np.abs(blocks).max(-1, keepdims=True)
    byte = np.maximum(np.where(amax > 0, np.frexp(amax)[1] - 1 + 127, 0) - down, 1)
    scale = np.exp2(byte - 127.0)
    codes = (blocks / scale).astype(np.float32).astype(dtype).astype(np.float64)
    return np.moveaxis((codes * scale).reshape(v.shape), -1, axis)


WIDE = False


def mx_kscale(k):
    if not WIDE:
        return np.ones(k)
    levels = np.array([10, -10, 5, -5, 0])
    if k % 512:
        return np.exp2(np.random.permutation(np.resize(levels, k // 32))).repeat(32)
    a = np.empty((k // 512, 16))
    for p in range(k // 512):
        a[p, :8] = np.random.permutation(np.resize(levels, 8))
        for g in range(8):
            far = levels[np.abs(levels - a[p, g]) >= 10]
            a[p, g + 8] = far[np.random.randint(len(far))]
    return np.exp2(a.ravel()).repeat(32)


def f64(x):
    return np.asarray(x).astype(np.float64)


def striped(idx):
    return np.tile(idx.reshape(-1, 16).T, (8, 1)).astype(np.uint16)


def unstriped(offs):
    return offs[:16].T.reshape(-1).astype(np.int64)


def striped8(idx):
    return np.concatenate([x.reshape(-1, 16).T for x in idx]).astype(np.uint16)


def runs(offs, k):
    lists = np.stack([offs[16 * r : 16 * r + 16].T.reshape(-1) for r in range(8)]).astype(np.int64)
    return lists[np.arange(k) % 512 // 64]


def pack_weight(w):
    k, n = w.shape
    w = f64(np.asarray(w, np.float32).astype(ml_dtypes.bfloat16)).reshape(k // 32, 32, n)
    amax = np.abs(w).max(1)
    byte = np.clip(np.where(amax > 0, np.frexp(amax)[1] - 1 + 127 - 7, 1), 1, 254)
    scaled = (w * np.exp2(127.0 - byte)[:, None, :]).reshape(k, n).astype(np.float32)
    words = np.ascontiguousarray(scaled.reshape(k // 512, 128, 4, n).transpose(0, 1, 3, 2)).astype(ml_dtypes.float8_e4m3fn).view(np.uint8)
    return words, np.ascontiguousarray(byte.astype(np.uint8).reshape(k // 512, 16, n))


def unpack_weight(words, scales):
    g, p, n, _ = words.shape
    vals = np.ascontiguousarray(words).view(ml_dtypes.float8_e4m3fn).astype(np.float64) * np.repeat(np.exp2(scales.astype(np.float64) - 127.0), 8, axis=1)[..., None]
    return vals.transpose(0, 1, 3, 2).reshape(g * 512, n)


def sigmoid(v):
    return 1.0 / (1.0 + np.exp(-np.maximum(v, -700.0)))


K, T, S, N, H, W = 512, 2048, 512, 512, 512, 256


def setup_inputs():
    n = np.random.standard_normal
    s = mx_kscale(K)[:, None]
    u = mx_kscale(S)
    packed_xT = pack_weight(n((K, T)) * s)
    perm = np.stack([np.random.permutation(N) for _ in range(8)])
    return {
        "x_words": packed_xT[0],
        "x_scales": packed_xT[1],
        "wa": (n((K, H)) / np.sqrt(K) / s).astype(np.float32),
        "wb": (n((K, N)) / np.sqrt(K) / s).astype(np.float32),
        "gt": (np.random.uniform(0.5, 1.5, (S, 1)) * u[:, None]).astype(np.float32),
        "gi": (np.random.uniform(0.5, 1.5, (S, 1)) / u[:, None]).astype(np.float32),
        "offs": striped(np.random.permutation(T)[:S]),
        "two": striped(np.random.permutation(T)[:S]),
        "n1": striped8(np.stack([np.random.permutation(H) for _ in range(8)])),
        "n2": striped8(np.stack([np.random.permutation(H) for _ in range(8)])),
        "n3": striped8(np.stack([np.random.permutation(H) for _ in range(8)])),
        "n4": striped8(perm[:, :W]),
        "n5": striped8(perm[:, W:]),
    }


def reference(x_words, x_scales, wa, wb, gt, gi, offs, two, n1, n2, n3, n4, n5):
    xq = unpack_weight(x_words, x_scales)[:, unstriped(offs)]
    a = xq.T @ mxq(f64(wa), 0, "e4m3")
    z = f64(gt) * ((a[np.arange(S)[:, None], runs(n1, S)]) * sigmoid(a) + (a[np.arange(S)[:, None], runs(n2, S)]) * (sigmoid(a[np.arange(S)[:, None], runs(n3, S)])))
    x_two = unpack_weight(x_words, x_scales)[:, unstriped(two)]
    b = x_two.T @ mxq(f64(wb), 0, "e4m3")
    z2 = f64(gi) * b
    cv = 0.0625 * ((mxq(z, 0, "e4m3").T @ mxq(z2, 0, "e4m3")))
    pa = cv[np.arange(H)[:, None], runs(n4, H)]
    pb = cv[np.arange(H)[:, None], runs(n5, H)]
    rb = np.maximum(pa, pb)
    ra = pa / (np.abs(pb) + 0.5)
    ds = np.zeros((H, N))
    ds[np.arange(H)[:, None], runs(n4, H)] = ra
    out = ds.copy()
    out[np.arange(H)[:, None], runs(n5, H)] = rb
    return out

@@ -1,0 +1,223 @@
+from contextlib import ExitStack
+
+import concourse.mybir as mybir
+from concourse.masks import make_identity
+
+K, T, S, N, H, W = 512, 2048, 512, 512, 512, 256
+FLOPS = 2 * K * S * H + 2 * K * S * N + 2 * S * H * N
+
+F32 = mybir.dt.float32
+BF16 = mybir.dt.bfloat16
+I32 = mybir.dt.int32
+U32 = mybir.dt.uint32
+U16 = mybir.dt.uint16
+U8 = mybir.dt.uint8
+FP8X4 = mybir.dt.float8_e4m3fn_x4
+ACT = mybir.ActivationFunctionType
+ALU = mybir.AluOpType
+
+P = 128
+PACK = 4
+RUN = 8
+HALF = 256
+FUSED = 2
+
+
+def tile_picked_momwsumratio_none_p_kernel(
+    tc, x_words, x_scales, wa, wb, gt, gi, offs, two, n1, n2, n3, n4, n5, out
+):
+    nc = tc.nc
+    with ExitStack() as ctx:
+        keep = ctx.enter_context(tc.tile_pool(name="keep", bufs=1))
+        psum = ctx.enter_context(tc.psum_pool(name="psum", bufs=1))
+
+        def load_list(name, dram, entries):
+            tile = keep.tile([P, entries // 16], U16, name=name)
+            nc.sync.dma_start(tile[:], dram)
+            return tile
+
+        def load_weight_half(name, w, h):
+            raw = keep.tile([P, PACK, HALF], F32, name=name, align_bytes=64)
+            nc.sync.dma_start(raw[:], w[:, h * HALF : (h + 1) * HALF].rearrange("(p j) n -> p j n", j=PACK))
+            return raw
+
+        scale_table = keep.tile([P, T], U8, name="scale_table")
+        nc.vector.memset(scale_table[:].bitcast(I32), 0)
+        gate_rows = keep.tile([P, P], F32, name="gate_rows")
+        nc.gpsimd.memset(gate_rows[:], 0.0)
+        identity = keep.tile([P, P], F32, name="identity")
+        make_identity(nc, identity[:])
+
+        offs_list = load_list("offs_list", offs, S)
+        word_table = keep.tile([P, T], U32, name="word_table")
+        nc.sync.dma_start(word_table[:].bitcast(I32), x_words[0].rearrange("p n t -> p (n t)").bitcast(I32))
+        for q in range(4):
+            nc.scalar.dma_start(
+                scale_table[32 * q : 32 * q + 4, :].bitcast(I32), x_scales[0, 4 * q : 4 * q + 4, :].bitcast(I32)
+            )
+        for r, gate in enumerate((gt, gi)):
+            nc.sync.dma_start(
+                gate_rows[PACK * r : PACK * (r + 1), :].rearrange("t (g i) -> t g i", i=RUN),
+                gate.rearrange("(g t i) o -> t g (i o)", t=PACK, i=RUN),
+            )
+        wa_raw = [load_weight_half(f"wa_raw{h}", wa, h) for h in range(2)]
+        two_list = load_list("two_list", two, S)
+        wb_raw = [load_weight_half(f"wb_raw{h}", wb, h) for h in range(2)]
+        n3_list = load_list("n3_list", n3, H)
+        n1_list = load_list("n1_list", n1, H)
+        n2_list = load_list("n2_list", n2, H)
+        n4_list = load_list("n4_list", n4, W)
+        n5_list = load_list("n5_list", n5, W)
+
+        def pick(name, dtype, table, offsets, tag):
+            picked = keep.tile([P, S], dtype, name=name, tag=tag, align_bytes=64)
+            nc.vector.tensor_copy(
+                picked[:].rearrange("p (t g i) -> p g t i", t=PACK, i=RUN), table[:].indirect(offsets[:])
+            )
+            return picked
+
+        def mx_tiles(name, width):
+            codes = keep.tile([P, width], U32, name=name + "_codes", align_bytes=64)
+            scales = keep.tile([P, width], U8, name=name + "_scales", align_bytes=64)
+            return codes, scales
+
+        def round_half(name, raw, copy, tag):
+            grouped = keep.tile([P, HALF, PACK], BF16, name=name, tag=tag, align_bytes=64)
+            copy(
+                grouped[:].rearrange("p (c i) t -> p c t i", i=4),
+                raw[:].rearrange("p t (c i) -> p c t i", i=4),
+            )
+            return grouped
+
+        def quantize(operand, cols, values):
+            codes, scales = operand
+            nc.vector.quantize_mx(out=codes[:, cols].bitcast(FP8X4), scales=scales[:, cols], in_=values)
+
+        def product(acc, stationary, m_cols, moving, n_cols):
+            nc.tensor.matmul_mx(
+                out=acc,
+                lhsT=stationary[0][:, m_cols].bitcast(FP8X4),
+                lhsT_scale=stationary[1][:, m_cols],
+                rhs=moving[0][:, n_cols].bitcast(FP8X4),
+                rhs_scale=moving[1][:, n_cols],
+                start=True,
+                stop=True,
+            )
+
+        def block(i, width):
+            return slice(i * width, (i + 1) * width)
+
+        gate_bank = psum.tile([P, P], F32, name="gate_bank", tag="bank7")
+        nc.tensor.transpose(gate_bank[:], gate_rows[:], identity[:])
+        gates = keep.tile([P, 2 * PACK], F32, name="gates")
+        nc.scalar.copy(gates[:], gate_bank[:, 0 : 2 * PACK])
+
+        xa = (
+            pick("xa_words", U32, word_table, offs_list, "xa_words"),
+            pick("xa_scales", U8, scale_table, offs_list, "xa_scales"),
+        )
+        xb_words = pick("xb_words", U32, word_table, two_list, "xb_words")
+        wa_mx = mx_tiles("wa", H)
+        wa_grouped = [round_half(f"wa_grouped{h}", wa_raw[h], nc.scalar.copy, f"grouped{h}") for h in range(2)]
+        for h in range(2):
+            quantize(wa_mx, block(h, HALF), wa_grouped[h][:].rearrange("p n t -> p (n t)"))
+
+        a_banks = []
+        for t in range(PACK):
+            bank = psum.tile([P, H], F32, name=f"a_bank{t}", tag=f"bank{t}")
+            product(bank[:], xa, block(t, P), wa_mx, slice(0, H))
+            a_banks.append(bank)
+
+        wb_mx = mx_tiles("wb", N)
+        wb_grouped = [round_half("wb_grouped0", wb_raw[0], nc.vector.tensor_copy, "grouped1")]
+        xb = (xb_words, pick("xb_scales", U8, scale_table, two_list, "wa_raw1"))
+        wb_grouped.append(round_half("wb_grouped1", wb_raw[1], nc.vector.tensor_copy, "grouped0"))
+        for h in range(2):
+            quantize(wb_mx, block(h, HALF), wb_grouped[h][:].rearrange("p n t -> p (n t)"))
+
+        b_banks = []
+        for c in range(N // P):
+            bank = psum.tile([P, PACK, P], F32, name=f"b_bank{c}", tag=f"bank{PACK + c}")
+            for t in range(PACK):
+                product(bank[:, t, :], xb, block(t, P), wb_mx, block(c, P))
+            b_banks.append(bank)
+
+        sig, weighted = [], []
+        for t in range(PACK):
+            sig.append(keep.tile([P, H], F32, name=f"sig{t}"))
+            nc.scalar.activation(sig[t][:], a_banks[t][:], ACT.Sigmoid)
+            weighted.append(keep.tile([P, H], F32, name=f"weighted{t}"))
+            nc.scalar.activation(weighted[t][:], a_banks[t][:], ACT.Copy, scale=gates[:, t : t + 1])
+
+        def fetch(name, window, offsets):
+            fetched = keep.tile([P, H], F32, name=name)
+            for h in range(2):
+                nc.scalar.activation(
+                    fetched[:, block(h, HALF)], window[:].indirect(offsets[:, block(h, HALF // 16)]), ACT.Copy
+                )
+            return fetched
+
+        def fetch_times(result, t, offsets, factor):
+            for h in range(2):
+                nc.vector.tensor_tensor(
+                    result[:, t, block(h, HALF)],
+                    weighted[t][:].indirect(offsets[:, block(h, HALF // 16)]),
+                    factor[:, block(h, HALF)],
+                    ALU.mult,
+                )
+
+        first = keep.tile([P, PACK, H], F32, name="first")
+        second = keep.tile([P, PACK, H], F32, name="second")
+        z2_grouped = keep.tile([P, N, PACK], BF16, name="z2_grouped", align_bytes=64)
+        for t in range(PACK):
+            fetch_times(first, t, n1_list, sig[t])
+            nc.vector.tensor_tensor(
+                z2_grouped[:, block(t, P), :],
+                b_banks[t][:].rearrange("p t n -> p n t"),
+                gates[:, PACK : 2 * PACK].unsqueeze(1).to_broadcast([P, P, PACK]),
+                ALU.mult,
+            )
+        for t in range(PACK):
+            sig_n3 = fetch(f"sig_n3_{t}", sig[t], n3_list)
+            if t < FUSED:
+                fetch_times(second, t, n2_list, sig_n3)
+            else:
+                weighted_n2 = fetch(f"weighted_n2_{t}", weighted[t], n2_list)
+                nc.vector.tensor_tensor(second[:, t, :], weighted_n2[:], sig_n3[:], ALU.mult)
+
+        z2_mx = mx_tiles("z2", N)
+        quantize(z2_mx, slice(0, N), z2_grouped[:].rearrange("p n t -> p (n t)"))
+
+        z_mx = mx_tiles("z", H)
+        for h in range(2):
+            grouped = keep.tile([P, 2, P, PACK], BF16, name=f"z_grouped{h}", tag="z_grouped", align_bytes=64)
+            nc.vector.tensor_tensor(
+                grouped[:].rearrange("p e m t -> p m t e"),
+                first[:].rearrange("p t (m h e) -> p h m t e", h=2, e=2)[:, h],
+                second[:].rearrange("p t (m h e) -> p h m t e", h=2, e=2)[:, h],
+                ALU.add,
+            )
+            quantize(z_mx, block(h, HALF), grouped[:].rearrange("p e m t -> p (e m t)"))
+
+        out_rows = out.rearrange("(p u) n -> u p n", u=PACK)
+        for u in range(PACK):
+            bank = psum.tile([P, N], F32, name=f"cv_bank{u}", tag=f"bank{u}")
+            product(bank[:], z_mx, block(u, P), z2_mx, slice(0, N))
+            cv = keep.tile([P, N], F32, name=f"cv{u}", tag="cv")
+            nc.scalar.activation(cv[:], bank[:], ACT.Copy, scale=0.0625)
+            pa = keep.tile([P, W], F32, name=f"pa{u}")
+            pb = keep.tile([P, W], F32, name=f"pb{u}")
+            nc.scalar.activation(pb[:], cv[:].indirect(n5_list[:]), ACT.Copy)
+            nc.scalar.activation(pa[:], cv[:].indirect(n4_list[:]), ACT.Copy)
+            size = keep.tile([P, W], F32, name=f"size{u}")
+            nc.scalar.activation(size[:], pb[:], ACT.Abs)
+            root = keep.tile([P, W], F32, name=f"root{u}")
+            nc.scalar.activation(root[:], size[:], ACT.Abs_reciprocal_sqrt, bias=0.5)
+            inverse = keep.tile([P, W], F32, name=f"inverse{u}")
+            nc.scalar.activation(inverse[:], root[:], ACT.Square)
+            rb = keep.tile([P, W], F32, name=f"rb{u}")
+            nc.vector.tensor_tensor(rb[:], pa[:], pb[:], ALU.max)
+            result = keep.tile([P, N], F32, name=f"result{u}")
+            nc.vector.tensor_copy(result[:].indirect(n5_list[:]), rb[:])
+            nc.vector.tensor_tensor(result[:].indirect(n4_list[:]), pa[:], inverse[:], ALU.mult)
+            nc.sync.dma_start(out_rows[u], result[:])

@@ -29,6 +29,7 @@ def tile_picked_momwsumratio_none_p_kernel(
     nc = tc.nc
     with ExitStack() as ctx:
         keep = ctx.enter_context(tc.tile_pool(name="keep", bufs=1))
+        stage = ctx.enter_context(tc.tile_pool(name="stage", bufs=1))
         psum = ctx.enter_context(tc.psum_pool(name="psum", bufs=1))
 
         def load_list(name, dram, entries):
@@ -36,58 +37,57 @@ def tile_picked_momwsumratio_none_p_kernel(
             nc.sync.dma_start(tile[:], dram)
             return tile
 
-        def load_weight_half(name, w, h):
-            raw = keep.tile([P, PACK, HALF], F32, name=name, align_bytes=64)
+        def load_weight_half(raw, w, h):
             nc.sync.dma_start(raw[:], w[:, h * HALF : (h + 1) * HALF].rearrange("(p j) n -> p j n", j=PACK))
             return raw
 
         scale_table = keep.tile([P, T], U8, name="scale_table")
-        nc.vector.memset(scale_table[:].bitcast(I32), 0)
+        nc.gpsimd.memset(scale_table[:].bitcast(I32), 0)
         gate_rows = keep.tile([P, P], F32, name="gate_rows")
         nc.gpsimd.memset(gate_rows[:], 0.0)
         identity = keep.tile([P, P], F32, name="identity")
         make_identity(nc, identity[:])
 
         offs_list = load_list("offs_list", offs, S)
+        two_list = load_list("two_list", two, S)
         word_table = keep.tile([P, T], U32, name="word_table")
         nc.sync.dma_start(word_table[:].bitcast(I32), x_words[0].rearrange("p n t -> p (n t)").bitcast(I32))
         for q in range(4):
-            nc.scalar.dma_start(
+            nc.sync.dma_start(
                 scale_table[32 * q : 32 * q + 4, :].bitcast(I32), x_scales[0, 4 * q : 4 * q + 4, :].bitcast(I32)
             )
+        wa_raw = [
+            load_weight_half(keep.tile([P, PACK, HALF], F32, name="wa_raw0"), wa, 0),
+            load_weight_half(stage.tile([P, PACK, HALF], F32, name="wa_raw1", offset=0, align_bytes=64), wa, 1),
+        ]
         for r, gate in enumerate((gt, gi)):
             nc.sync.dma_start(
                 gate_rows[PACK * r : PACK * (r + 1), :].rearrange("t (g i) -> t g i", i=RUN),
                 gate.rearrange("(g t i) o -> t g (i o)", t=PACK, i=RUN),
             )
-        wa_raw = [load_weight_half(f"wa_raw{h}", wa, h) for h in range(2)]
-        two_list = load_list("two_list", two, S)
-        wb_raw = [load_weight_half(f"wb_raw{h}", wb, h) for h in range(2)]
+        wb_raw = [load_weight_half(keep.tile([P, PACK, HALF], F32, name=f"wb_raw{h}"), wb, h) for h in range(2)]
         n3_list = load_list("n3_list", n3, H)
         n1_list = load_list("n1_list", n1, H)
         n2_list = load_list("n2_list", n2, H)
         n4_list = load_list("n4_list", n4, W)
         n5_list = load_list("n5_list", n5, W)
 
-        def pick(name, dtype, table, offsets, tag):
-            picked = keep.tile([P, S], dtype, name=name, tag=tag, align_bytes=64)
+        def pick(picked, table, offsets):
             nc.vector.tensor_copy(
                 picked[:].rearrange("p (t g i) -> p g t i", t=PACK, i=RUN), table[:].indirect(offsets[:])
             )
             return picked
 
-        def mx_tiles(name, width):
-            codes = keep.tile([P, width], U32, name=name + "_codes", align_bytes=64)
+        def mx_tiles(name, width, tag=None):
+            codes = keep.tile([P, width], U32, name=name + "_codes", tag=tag or name + "_codes", align_bytes=64)
             scales = keep.tile([P, width], U8, name=name + "_scales", align_bytes=64)
             return codes, scales
 
-        def round_half(name, raw, copy, tag):
-            grouped = keep.tile([P, HALF, PACK], BF16, name=name, tag=tag, align_bytes=64)
+        def round_half(grouped, raw, copy):
             copy(
-                grouped[:].rearrange("p (c i) t -> p c t i", i=4),
+                grouped.rearrange("p (c i) t -> p c t i", i=4),
                 raw[:].rearrange("p t (c i) -> p c t i", i=4),
             )
-            return grouped
 
         def quantize(operand, cols, values):
             codes, scales = operand
@@ -107,20 +107,22 @@ def tile_picked_momwsumratio_none_p_kernel(
         def block(i, width):
             return slice(i * width, (i + 1) * width)
 
-        gate_bank = psum.tile([P, P], F32, name="gate_bank", tag="bank7")
-        nc.tensor.transpose(gate_bank[:], gate_rows[:], identity[:])
-        gates = keep.tile([P, 2 * PACK], F32, name="gates")
-        nc.scalar.copy(gates[:], gate_bank[:, 0 : 2 * PACK])
-
         xa = (
-            pick("xa_words", U32, word_table, offs_list, "xa_words"),
-            pick("xa_scales", U8, scale_table, offs_list, "xa_scales"),
+            pick(keep.tile([P, S], U32, name="xa_words", align_bytes=64), word_table, offs_list),
+            pick(keep.tile([P, S], U8, name="xa_scales", align_bytes=64), scale_table, offs_list),
         )
-        xb_words = pick("xb_words", U32, word_table, two_list, "xb_words")
+        xb_words = pick(keep.tile([P, S], U32, name="xb_words", align_bytes=64), word_table, two_list)
         wa_mx = mx_tiles("wa", H)
-        wa_grouped = [round_half(f"wa_grouped{h}", wa_raw[h], nc.scalar.copy, f"grouped{h}") for h in range(2)]
+        wa_grouped = [keep.tile([P, HALF, PACK], BF16, name=f"wa_grouped{h}", align_bytes=64) for h in range(2)]
+        for h in range(2):
+            round_half(wa_grouped[h][:], wa_raw[h], nc.scalar.copy)
         for h in range(2):
             quantize(wa_mx, block(h, HALF), wa_grouped[h][:].rearrange("p n t -> p (n t)"))
+
+        gate_bank = psum.tile([P, P], F32, name="gate_bank", tag="bank7")
+        nc.tensor.transpose(gate_bank[:], gate_rows[:], identity[:])
+        gates = stage.tile([P, 2 * PACK], F32, name="gates", offset=S, align_bytes=64)
+        nc.scalar.copy(gates[:], gate_bank[:, 0 : 2 * PACK])
 
         a_banks = []
         for t in range(PACK):
@@ -129,11 +131,12 @@ def tile_picked_momwsumratio_none_p_kernel(
             a_banks.append(bank)
 
         wb_mx = mx_tiles("wb", N)
-        wb_grouped = [round_half("wb_grouped0", wb_raw[0], nc.vector.tensor_copy, "grouped1")]
-        xb = (xb_words, pick("xb_scales", U8, scale_table, two_list, "wa_raw1"))
-        wb_grouped.append(round_half("wb_grouped1", wb_raw[1], nc.vector.tensor_copy, "grouped0"))
+        wb_grouped = keep.tile([P, N, PACK], BF16, name="wb_grouped", tag="wa_grouped1", align_bytes=64)
+        round_half(wb_grouped[:, block(0, HALF), :], wb_raw[0], nc.vector.tensor_copy)
+        xb = (xb_words, pick(stage.tile([P, S], U8, name="xb_scales", offset=0, align_bytes=64), scale_table, two_list))
+        round_half(wb_grouped[:, block(1, HALF), :], wb_raw[1], nc.vector.tensor_copy)
         for h in range(2):
-            quantize(wb_mx, block(h, HALF), wb_grouped[h][:].rearrange("p n t -> p (n t)"))
+            quantize(wb_mx, block(h, HALF), wb_grouped[:, block(h, HALF), :].rearrange("p n t -> p (n t)"))
 
         b_banks = []
         for c in range(N // P):
@@ -146,7 +149,7 @@ def tile_picked_momwsumratio_none_p_kernel(
         for t in range(PACK):
             sig.append(keep.tile([P, H], F32, name=f"sig{t}"))
             nc.scalar.activation(sig[t][:], a_banks[t][:], ACT.Sigmoid)
-            weighted.append(keep.tile([P, H], F32, name=f"weighted{t}"))
+            weighted.append(keep.tile([P, H], F32, name=f"weighted{t}", align_bytes=64))
             nc.scalar.activation(weighted[t][:], a_banks[t][:], ACT.Copy, scale=gates[:, t : t + 1])
 
         def fetch(name, window, offsets):
@@ -189,35 +192,51 @@ def tile_picked_momwsumratio_none_p_kernel(
         quantize(z2_mx, slice(0, N), z2_grouped[:].rearrange("p n t -> p (n t)"))
 
         z_mx = mx_tiles("z", H)
-        for h in range(2):
-            grouped = keep.tile([P, 2, P, PACK], BF16, name=f"z_grouped{h}", tag="z_grouped", align_bytes=64)
+
+        def add_terms(grouped, u):
             nc.vector.tensor_tensor(
-                grouped[:].rearrange("p e m t -> p m t e"),
-                first[:].rearrange("p t (m h e) -> p h m t e", h=2, e=2)[:, h],
-                second[:].rearrange("p t (m h e) -> p h m t e", h=2, e=2)[:, h],
+                grouped.rearrange("p (c i) t -> p c t i", i=4),
+                first[:].rearrange("p t (c u i) -> p u c t i", u=PACK, i=4)[:, u],
+                second[:].rearrange("p t (c u i) -> p u c t i", u=PACK, i=4)[:, u],
                 ALU.add,
             )
-            quantize(z_mx, block(h, HALF), grouped[:].rearrange("p e m t -> p (e m t)"))
 
-        out_rows = out.rearrange("(p u) n -> u p n", u=PACK)
-        for u in range(PACK):
-            bank = psum.tile([P, N], F32, name=f"cv_bank{u}", tag=f"bank{u}")
+        z_head = keep.tile([P, P, PACK], BF16, name="z_head", tag="z_grouped", align_bytes=64)
+        add_terms(z_head[:], 0)
+        quantize(z_mx, block(0, P), z_head[:].rearrange("p m t -> p (m t)"))
+        z_rest = keep.tile([P, H - P, PACK], BF16, name="z_rest", tag="z_grouped", align_bytes=64)
+        for u in range(1, PACK):
+            add_terms(z_rest[:, block(u - 1, P), :], u)
+        quantize(z_mx, slice(P, H), z_rest[:].rearrange("p m t -> p (m t)"))
+
+        out_rows = out.rearrange("(c u i) n -> u c i n", u=PACK, i=4)
+        pa, pb, result = [], [], []
+
+        def put_larger(u):
+            bank = psum.tile([P, N], F32, name=f"cv_bank{u}", tag="bank0")
             product(bank[:], z_mx, block(u, P), z2_mx, slice(0, N))
-            cv = keep.tile([P, N], F32, name=f"cv{u}", tag="cv")
+            cv = keep.tile([P, N], F32, name=f"cv{u}")
             nc.scalar.activation(cv[:], bank[:], ACT.Copy, scale=0.0625)
-            pa = keep.tile([P, W], F32, name=f"pa{u}")
-            pb = keep.tile([P, W], F32, name=f"pb{u}")
-            nc.scalar.activation(pb[:], cv[:].indirect(n5_list[:]), ACT.Copy)
-            nc.scalar.activation(pa[:], cv[:].indirect(n4_list[:]), ACT.Copy)
+            pa.append(keep.tile([P, W], F32, name=f"pa{u}"))
+            pb.append(keep.tile([P, W], F32, name=f"pb{u}"))
+            nc.scalar.activation(pb[u][:], cv[:].indirect(n5_list[:]), ACT.Copy)
+            nc.scalar.activation(pa[u][:], cv[:].indirect(n4_list[:]), ACT.Copy)
+            rb = keep.tile([P, W], F32, name=f"rb{u}")
+            nc.vector.tensor_tensor(rb[:], pa[u][:], pb[u][:], ALU.max)
+            result.append(keep.tile([P, N], F32, name=f"result{u}"))
+            nc.vector.tensor_copy(result[u][:].indirect(n5_list[:]), rb[:])
+
+        def put_ratio(u):
             size = keep.tile([P, W], F32, name=f"size{u}")
-            nc.scalar.activation(size[:], pb[:], ACT.Abs)
-            root = keep.tile([P, W], F32, name=f"root{u}")
+            nc.scalar.activation(size[:], pb[u][:], ACT.Abs)
+            root = keep.tile([P, W], F32, name=f"root{u}", tag=f"cv{PACK - 1}")
             nc.scalar.activation(root[:], size[:], ACT.Abs_reciprocal_sqrt, bias=0.5)
             inverse = keep.tile([P, W], F32, name=f"inverse{u}")
             nc.scalar.activation(inverse[:], root[:], ACT.Square)
-            rb = keep.tile([P, W], F32, name=f"rb{u}")
-            nc.vector.tensor_tensor(rb[:], pa[:], pb[:], ALU.max)
-            result = keep.tile([P, N], F32, name=f"result{u}")
-            nc.vector.tensor_copy(result[:].indirect(n5_list[:]), rb[:])
-            nc.vector.tensor_tensor(result[:].indirect(n4_list[:]), pa[:], inverse[:], ALU.mult)
-            nc.sync.dma_start(out_rows[u], result[:])
+            nc.vector.tensor_tensor(result[u][:].indirect(n4_list[:]), pa[u][:], inverse[:], ALU.mult)
+            nc.sync.dma_start(out_rows[u], result[u][:])
+
+        for u in range(PACK):
+            put_larger(u)
+        for u in range(PACK):
+            put_ratio(u)

from contextlib import ExitStack

import concourse.mybir as mybir
from concourse.masks import make_identity

K, T, S, N, H, W = 512, 2048, 512, 512, 512, 256
FLOPS = 2 * K * S * H + 2 * K * S * N + 2 * S * H * N

F32 = mybir.dt.float32
BF16 = mybir.dt.bfloat16
I32 = mybir.dt.int32
U32 = mybir.dt.uint32
U16 = mybir.dt.uint16
U8 = mybir.dt.uint8
FP8X4 = mybir.dt.float8_e4m3fn_x4
ACT = mybir.ActivationFunctionType
ALU = mybir.AluOpType

P = 128
PACK = 4
RUN = 8
HALF = 256
FUSED = 2


def tile_picked_momwsumratio_none_p_kernel(
    tc, x_words, x_scales, wa, wb, gt, gi, offs, two, n1, n2, n3, n4, n5, out
):
    nc = tc.nc
    with ExitStack() as ctx:
        keep = ctx.enter_context(tc.tile_pool(name="keep", bufs=1))
        stage = ctx.enter_context(tc.tile_pool(name="stage", bufs=1))
        psum = ctx.enter_context(tc.psum_pool(name="psum", bufs=1))

        def load_list(name, dram, entries):
            tile = keep.tile([P, entries // 16], U16, name=name)
            nc.sync.dma_start(tile[:], dram)
            return tile

        def load_weight_half(raw, w, h):
            nc.sync.dma_start(raw[:], w[:, h * HALF : (h + 1) * HALF].rearrange("(p j) n -> p j n", j=PACK))
            return raw

        scale_table = keep.tile([P, T], U8, name="scale_table")
        nc.gpsimd.memset(scale_table[:].bitcast(I32), 0)
        gate_rows = keep.tile([P, P], F32, name="gate_rows")
        nc.gpsimd.memset(gate_rows[:], 0.0)
        identity = keep.tile([P, P], F32, name="identity")
        make_identity(nc, identity[:])

        offs_list = load_list("offs_list", offs, S)
        two_list = load_list("two_list", two, S)
        word_table = keep.tile([P, T], U32, name="word_table")
        nc.sync.dma_start(word_table[:].bitcast(I32), x_words[0].rearrange("p n t -> p (n t)").bitcast(I32))
        for q in range(4):
            nc.sync.dma_start(
                scale_table[32 * q : 32 * q + 4, :].bitcast(I32), x_scales[0, 4 * q : 4 * q + 4, :].bitcast(I32)
            )
        wa_raw = [
            load_weight_half(keep.tile([P, PACK, HALF], F32, name="wa_raw0"), wa, 0),
            load_weight_half(stage.tile([P, PACK, HALF], F32, name="wa_raw1", offset=0, align_bytes=64), wa, 1),
        ]
        for r, gate in enumerate((gt, gi)):
            nc.sync.dma_start(
                gate_rows[PACK * r : PACK * (r + 1), :].rearrange("t (g i) -> t g i", i=RUN),
                gate.rearrange("(g t i) o -> t g (i o)", t=PACK, i=RUN),
            )
        wb_raw = [load_weight_half(keep.tile([P, PACK, HALF], F32, name=f"wb_raw{h}"), wb, h) for h in range(2)]
        n3_list = load_list("n3_list", n3, H)
        n1_list = load_list("n1_list", n1, H)
        n2_list = load_list("n2_list", n2, H)
        n4_list = load_list("n4_list", n4, W)
        n5_list = load_list("n5_list", n5, W)

        def pick(picked, table, offsets):
            nc.vector.tensor_copy(
                picked[:].rearrange("p (t g i) -> p g t i", t=PACK, i=RUN), table[:].indirect(offsets[:])
            )
            return picked

        def mx_tiles(name, width, tag=None):
            codes = keep.tile([P, width], U32, name=name + "_codes", tag=tag or name + "_codes", align_bytes=64)
            scales = keep.tile([P, width], U8, name=name + "_scales", align_bytes=64)
            return codes, scales

        def round_half(grouped, raw, copy):
            copy(
                grouped.rearrange("p (c i) t -> p c t i", i=4),
                raw[:].rearrange("p t (c i) -> p c t i", i=4),
            )

        def quantize(operand, cols, values):
            codes, scales = operand
            nc.vector.quantize_mx(out=codes[:, cols].bitcast(FP8X4), scales=scales[:, cols], in_=values)

        def product(acc, stationary, m_cols, moving, n_cols):
            nc.tensor.matmul_mx(
                out=acc,
                lhsT=stationary[0][:, m_cols].bitcast(FP8X4),
                lhsT_scale=stationary[1][:, m_cols],
                rhs=moving[0][:, n_cols].bitcast(FP8X4),
                rhs_scale=moving[1][:, n_cols],
                start=True,
                stop=True,
            )

        def block(i, width):
            return slice(i * width, (i + 1) * width)

        xa = (
            pick(keep.tile([P, S], U32, name="xa_words", align_bytes=64), word_table, offs_list),
            pick(keep.tile([P, S], U8, name="xa_scales", align_bytes=64), scale_table, offs_list),
        )
        xb_words = pick(keep.tile([P, S], U32, name="xb_words", align_bytes=64), word_table, two_list)
        wa_mx = mx_tiles("wa", H)
        wa_grouped = [keep.tile([P, HALF, PACK], BF16, name=f"wa_grouped{h}", align_bytes=64) for h in range(2)]
        for h in range(2):
            round_half(wa_grouped[h][:], wa_raw[h], nc.scalar.copy)
        for h in range(2):
            quantize(wa_mx, block(h, HALF), wa_grouped[h][:].rearrange("p n t -> p (n t)"))

        gate_bank = psum.tile([P, P], F32, name="gate_bank", tag="bank7")
        nc.tensor.transpose(gate_bank[:], gate_rows[:], identity[:])
        gates = stage.tile([P, 2 * PACK], F32, name="gates", offset=S, align_bytes=64)
        nc.scalar.copy(gates[:], gate_bank[:, 0 : 2 * PACK])

        a_banks = []
        for t in range(PACK):
            bank = psum.tile([P, H], F32, name=f"a_bank{t}", tag=f"bank{t}")
            product(bank[:], xa, block(t, P), wa_mx, slice(0, H))
            a_banks.append(bank)

        wb_mx = mx_tiles("wb", N)
        wb_grouped = keep.tile([P, N, PACK], BF16, name="wb_grouped", tag="wa_grouped1", align_bytes=64)
        round_half(wb_grouped[:, block(0, HALF), :], wb_raw[0], nc.vector.tensor_copy)
        xb = (xb_words, pick(stage.tile([P, S], U8, name="xb_scales", offset=0, align_bytes=64), scale_table, two_list))
        round_half(wb_grouped[:, block(1, HALF), :], wb_raw[1], nc.vector.tensor_copy)
        for h in range(2):
            quantize(wb_mx, block(h, HALF), wb_grouped[:, block(h, HALF), :].rearrange("p n t -> p (n t)"))

        b_banks = []
        for c in range(N // P):
            bank = psum.tile([P, PACK, P], F32, name=f"b_bank{c}", tag=f"bank{PACK + c}")
            for t in range(PACK):
                product(bank[:, t, :], xb, block(t, P), wb_mx, block(c, P))
            b_banks.append(bank)

        sig, weighted = [], []
        for t in range(PACK):
            sig.append(keep.tile([P, H], F32, name=f"sig{t}"))
            nc.scalar.activation(sig[t][:], a_banks[t][:], ACT.Sigmoid)
            weighted.append(keep.tile([P, H], F32, name=f"weighted{t}", align_bytes=64))
            nc.scalar.activation(weighted[t][:], a_banks[t][:], ACT.Copy, scale=gates[:, t : t + 1])

        def fetch(name, window, offsets):
            fetched = keep.tile([P, H], F32, name=name)
            for h in range(2):
                nc.scalar.activation(
                    fetched[:, block(h, HALF)], window[:].indirect(offsets[:, block(h, HALF // 16)]), ACT.Copy
                )
            return fetched

        def fetch_times(result, t, offsets, factor):
            for h in range(2):
                nc.vector.tensor_tensor(
                    result[:, t, block(h, HALF)],
                    weighted[t][:].indirect(offsets[:, block(h, HALF // 16)]),
                    factor[:, block(h, HALF)],
                    ALU.mult,
                )

        first = keep.tile([P, PACK, H], F32, name="first")
        second = keep.tile([P, PACK, H], F32, name="second")
        z2_grouped = keep.tile([P, N, PACK], BF16, name="z2_grouped", align_bytes=64)
        for t in range(PACK):
            fetch_times(first, t, n1_list, sig[t])
            nc.vector.tensor_tensor(
                z2_grouped[:, block(t, P), :],
                b_banks[t][:].rearrange("p t n -> p n t"),
                gates[:, PACK : 2 * PACK].unsqueeze(1).to_broadcast([P, P, PACK]),
                ALU.mult,
            )
        for t in range(PACK):
            sig_n3 = fetch(f"sig_n3_{t}", sig[t], n3_list)
            if t < FUSED:
                fetch_times(second, t, n2_list, sig_n3)
            else:
                weighted_n2 = fetch(f"weighted_n2_{t}", weighted[t], n2_list)
                nc.vector.tensor_tensor(second[:, t, :], weighted_n2[:], sig_n3[:], ALU.mult)

        z2_mx = mx_tiles("z2", N)
        quantize(z2_mx, slice(0, N), z2_grouped[:].rearrange("p n t -> p (n t)"))

        z_mx = mx_tiles("z", H)

        def add_terms(grouped, u):
            nc.vector.tensor_tensor(
                grouped.rearrange("p (c i) t -> p c t i", i=4),
                first[:].rearrange("p t (c u i) -> p u c t i", u=PACK, i=4)[:, u],
                second[:].rearrange("p t (c u i) -> p u c t i", u=PACK, i=4)[:, u],
                ALU.add,
            )

        z_head = keep.tile([P, P, PACK], BF16, name="z_head", tag="z_grouped", align_bytes=64)
        add_terms(z_head[:], 0)
        quantize(z_mx, block(0, P), z_head[:].rearrange("p m t -> p (m t)"))
        z_rest = keep.tile([P, H - P, PACK], BF16, name="z_rest", tag="z_grouped", align_bytes=64)
        for u in range(1, PACK):
            add_terms(z_rest[:, block(u - 1, P), :], u)
        quantize(z_mx, slice(P, H), z_rest[:].rearrange("p m t -> p (m t)"))

        out_rows = out.rearrange("(c u i) n -> u c i n", u=PACK, i=4)
        pa, pb, result = [], [], []

        def put_larger(u):
            bank = psum.tile([P, N], F32, name=f"cv_bank{u}", tag="bank0")
            product(bank[:], z_mx, block(u, P), z2_mx, slice(0, N))
            cv = keep.tile([P, N], F32, name=f"cv{u}")
            nc.scalar.activation(cv[:], bank[:], ACT.Copy, scale=0.0625)
            pa.append(keep.tile([P, W], F32, name=f"pa{u}"))
            pb.append(keep.tile([P, W], F32, name=f"pb{u}"))
            nc.scalar.activation(pb[u][:], cv[:].indirect(n5_list[:]), ACT.Copy)
            nc.scalar.activation(pa[u][:], cv[:].indirect(n4_list[:]), ACT.Copy)
            rb = keep.tile([P, W], F32, name=f"rb{u}")
            nc.vector.tensor_tensor(rb[:], pa[u][:], pb[u][:], ALU.max)
            result.append(keep.tile([P, N], F32, name=f"result{u}"))
            nc.vector.tensor_copy(result[u][:].indirect(n5_list[:]), rb[:])

        def put_ratio(u):
            size = keep.tile([P, W], F32, name=f"size{u}")
            nc.scalar.activation(size[:], pb[u][:], ACT.Abs)
            root = keep.tile([P, W], F32, name=f"root{u}", tag=f"cv{PACK - 1}")
            nc.scalar.activation(root[:], size[:], ACT.Abs_reciprocal_sqrt, bias=0.5)
            inverse = keep.tile([P, W], F32, name=f"inverse{u}")
            nc.scalar.activation(inverse[:], root[:], ACT.Square)
            nc.vector.tensor_tensor(result[u][:].indirect(n4_list[:]), pa[u][:], inverse[:], ALU.mult)
            nc.sync.dma_start(out_rows[u], result[u][:])

        for u in range(PACK):
            put_larger(u)
        for u in range(PACK):
            put_ratio(u)
